import numpy as np
import ml_dtypes


def mxq(x, axis, fmt="e4m3"):
    dtype, down = {"e4m3": (ml_dtypes.float8_e4m3fn, 7), "e5m2": (ml_dtypes.float8_e5m2, 14)}[fmt]
    v = np.moveaxis(np.asarray(x, np.float32).astype(ml_dtypes.bfloat16).astype(np.float64), axis, -1)
    blocks = v.reshape(v.shape[:-1] + (-1, 32))
    amax = np.abs(blocks).max(-1, keepdims=True)
    byte = np.maximum(np.where(amax > 0, np.frexp(amax)[1] - 1 + 127, 0) - down, 1)
    scale = np.exp2(byte - 127.0)
    codes = (blocks / scale).astype(np.float32).astype(dtype).astype(np.float64)
    return np.moveaxis((codes * scale).reshape(v.shape), -1, axis)


WIDE = False


def mx_kscale(k):
    if not WIDE:
        return np.ones(k)
    levels = np.array([10, -10, 5, -5, 0])
    if k % 512:
        return np.exp2(np.random.permutation(np.resize(levels, k // 32))).repeat(32)
    a = np.empty((k // 512, 16))
    for p in range(k // 512):
        a[p, :8] = np.random.permutation(np.resize(levels, 8))
        for g in range(8):
            far = levels[np.abs(levels - a[p, g]) >= 10]
            a[p, g + 8] = far[np.random.randint(len(far))]
    return np.exp2(a.ravel()).repeat(32)


def f64(x):
    return np.asarray(x).astype(np.float64)


def striped(idx):
    return np.tile(idx.reshape(-1, 16).T, (8, 1)).astype(np.uint16)


def unstriped(offs):
    return offs[:16].T.reshape(-1).astype(np.int64)


def pack_weight(w):
    k, n = w.shape
    w = f64(np.asarray(w, np.float32).astype(ml_dtypes.bfloat16)).reshape(k // 32, 32, n)
    amax = np.abs(w).max(1)
    byte = np.clip(np.where(amax > 0, np.frexp(amax)[1] - 1 + 127 - 7, 1), 1, 254)
    scaled = (w * np.exp2(127.0 - byte)[:, None, :]).reshape(k, n).astype(np.float32)
    words = np.ascontiguousarray(scaled.reshape(k // 512, 128, 4, n).transpose(0, 1, 3, 2)).astype(ml_dtypes.float8_e4m3fn).view(np.uint8)
    return words, np.ascontiguousarray(byte.astype(np.uint8).reshape(k // 512, 16, n))


def unpack_weight(words, scales):
    g, p, n, _ = words.shape
    vals = np.ascontiguousarray(words).view(ml_dtypes.float8_e4m3fn).astype(np.float64) * np.repeat(np.exp2(scales.astype(np.float64) - 127.0), 8, axis=1)[..., None]
    return vals.transpose(0, 1, 3, 2).reshape(g * 512, n)


def silu(v):
    return v / (1.0 + np.exp(-np.maximum(v, -700.0)))


K, T, S, N = 512, 4096, 1024, 128


def setup_inputs():
    n = np.random.standard_normal
    s = mx_kscale(K)[:, None]
    packed_w1 = pack_weight(n((K, N)) / np.sqrt(K) / s)
    return {
        "xT": (n((K, T)) * s).astype(np.float32),
        "side": n((N, T)).astype(np.float32),
        "w1_words": packed_w1[0],
        "w1_scales": packed_w1[1],
        "offs": striped(np.random.permutation(T)[:S]),
    }


def reference(xT, side, w1_words, w1_scales, offs):
    xq = mxq(f64(xT)[:, unstriped(offs)], 0, "e4m3")
    y = unpack_weight(w1_words, w1_scales).T @ xq
    g = f64(side)[:, unstriped(offs)]
    return y * silu(g)

@@ -1,0 +1,79 @@
+from contextlib import ExitStack
+
+import concourse.mybir as mybir
+
+K, T, S, N = 512, 4096, 1024, 128
+FLOPS = 2 * K * N * S
+
+F32 = mybir.dt.float32
+BF16 = mybir.dt.bfloat16
+I32 = mybir.dt.int32
+U32 = mybir.dt.uint32
+U16 = mybir.dt.uint16
+U8 = mybir.dt.uint8
+FP8X4 = mybir.dt.float8_e4m3fn_x4
+SILU = mybir.ActivationFunctionType.Silu
+MULT = mybir.AluOpType.mult
+
+P = 128
+PACK = 4
+HALF = 512
+PIECE = 256
+LIST_ROWS = 16
+
+
+def tile_picked_sidegate_silu_l_kernel(tc, xT, side, w1_words, w1_scales, offs, out):
+    nc = tc.nc
+    halves = range(S // HALF)
+    with ExitStack() as ctx:
+        held = ctx.enter_context(tc.tile_pool(name="held", bufs=1))
+        psum = ctx.enter_context(tc.psum_pool(name="psum", bufs=1))
+
+        offsets = held.tile([P, S // LIST_ROWS], U16, name="offsets")
+        planes = [held.tile([P, T], F32, name=f"plane{t}") for t in range(PACK)]
+        side_rows = held.tile([P, T], F32, name="side_rows")
+        w_codes = held.tile([P, N], U32, name="w_codes", align_bytes=64)
+        w_scales = held.tile([P, N], U8, name="w_scales", align_bytes=64)
+
+        x_rows = xT.rearrange("(p t) w -> p t w", t=PACK)
+        nc.sync.dma_start(out=planes[0][:], in_=x_rows[:, 0, :])
+        nc.sync.dma_start(offsets[:], offs)
+        nc.sync.dma_start(out=w_codes[:].bitcast(I32), in_=w1_words[0].rearrange("p n t -> p (n t)").bitcast(I32))
+        for t in range(1, PACK):
+            nc.sync.dma_start(out=planes[t][:], in_=x_rows[:, t, :])
+        nc.sync.dma_start(out=side_rows[:], in_=side)
+
+        nc.gpsimd.memset(w_scales[:].bitcast(I32), 0)
+        for q in range(4):
+            nc.gpsimd.dma_start(out=w_scales[32 * q : 32 * q + 4, :].bitcast(I32),
+                                in_=w1_scales[0, 4 * q : 4 * q + 4, :].bitcast(I32))
+
+        def entries(h):
+            return offsets[:, h * HALF // LIST_ROWS : (h + 1) * HALF // LIST_ROWS]
+
+        grouped = [held.tile([P, HALF, PACK], BF16, name=f"grouped{h}", align_bytes=64) for h in halves]
+        for t in range(PACK):
+            for h in halves:
+                nc.vector.tensor_copy(grouped[h][:, :, t], planes[t][:].indirect(entries(h)))
+
+        products = []
+        for h in halves:
+            codes = held.tile([P, HALF], U32, name=f"codes{h}", align_bytes=64)
+            scales = held.tile([P, HALF], U8, name=f"scales{h}", align_bytes=64)
+            nc.vector.quantize_mx(out=codes[:].bitcast(FP8X4), scales=scales[:],
+                                  in_=grouped[h][:].rearrange("p n t -> p (n t)"))
+            y = psum.tile([N, HALF], F32, name=f"y{h}")
+            nc.tensor.matmul_mx(out=y[:], lhsT=w_codes[:].bitcast(FP8X4), lhsT_scale=w_scales[:],
+                                rhs=codes[:].bitcast(FP8X4), rhs_scale=scales[:], start=True, stop=True)
+            products.append(y)
+
+        picked = [held.tile([P, HALF], F32, name=f"picked{h}") for h in halves]
+        for h in halves:
+            nc.vector.tensor_copy(picked[h][:], side_rows[:].indirect(entries(h)))
+        for i in range(S // PIECE):
+            h, c0 = divmod(i * PIECE, HALF)
+            gate = held.tile([P, PIECE], F32, name=f"gate{i}")
+            nc.scalar.activation(gate[:], picked[h][:, c0 : c0 + PIECE], SILU)
+            result = held.tile([P, PIECE], F32, name=f"result{i}")
+            nc.vector.tensor_tensor(result[:], products[h][:, c0 : c0 + PIECE], gate[:], MULT)
+            nc.sync.dma_start(out=out[:, i * PIECE : (i + 1) * PIECE], in_=result[:])

@@ -43,9 +43,9 @@ def tile_picked_sidegate_silu_l_kernel(tc, xT, side, w1_words, w1_scales, offs, 
             nc.sync.dma_start(out=planes[t][:], in_=x_rows[:, t, :])
         nc.sync.dma_start(out=side_rows[:], in_=side)
 
-        nc.gpsimd.memset(w_scales[:].bitcast(I32), 0)
+        nc.vector.memset(w_scales[:].bitcast(I32), 0)
         for q in range(4):
-            nc.gpsimd.dma_start(out=w_scales[32 * q : 32 * q + 4, :].bitcast(I32),
+            nc.scalar.dma_start(out=w_scales[32 * q : 32 * q + 4, :].bitcast(I32),
                                 in_=w1_scales[0, 4 * q : 4 * q + 4, :].bitcast(I32))
 
         def entries(h):
@@ -53,8 +53,10 @@ def tile_picked_sidegate_silu_l_kernel(tc, xT, side, w1_words, w1_scales, offs, 
 
         grouped = [held.tile([P, HALF, PACK], BF16, name=f"grouped{h}", align_bytes=64) for h in halves]
         for t in range(PACK):
-            for h in halves:
-                nc.vector.tensor_copy(grouped[h][:, :, t], planes[t][:].indirect(entries(h)))
+            dense = held.tile([P, HALF], F32, name=f"dense{t}")
+            nc.vector.tensor_copy(dense[:], planes[t][:].indirect(entries(0)))
+            nc.scalar.copy(grouped[0][:, :, t], dense[:])
+            nc.vector.tensor_copy(grouped[1][:, :, t], planes[t][:].indirect(entries(1)))
 
         products = []
         for h in halves:

@@ -38,14 +38,14 @@ def tile_picked_sidegate_silu_l_kernel(tc, xT, side, w1_words, w1_scales, offs, 
         x_rows = xT.rearrange("(p t) w -> p t w", t=PACK)
         nc.sync.dma_start(out=planes[0][:], in_=x_rows[:, 0, :])
         nc.sync.dma_start(offsets[:], offs)
-        nc.sync.dma_start(out=w_codes[:].bitcast(I32), in_=w1_words[0].rearrange("p n t -> p (n t)").bitcast(I32))
         for t in range(1, PACK):
             nc.sync.dma_start(out=planes[t][:], in_=x_rows[:, t, :])
         nc.sync.dma_start(out=side_rows[:], in_=side)
+        nc.sync.dma_start(out=w_codes[:].bitcast(I32), in_=w1_words[0].rearrange("p n t -> p (n t)").bitcast(I32))
 
         nc.vector.memset(w_scales[:].bitcast(I32), 0)
         for q in range(4):
-            nc.scalar.dma_start(out=w_scales[32 * q : 32 * q + 4, :].bitcast(I32),
+            nc.sync.dma_start(out=w_scales[32 * q : 32 * q + 4, :].bitcast(I32),
                                 in_=w1_scales[0, 4 * q : 4 * q + 4, :].bitcast(I32))
 
         def entries(h):

@@ -45,7 +45,7 @@ def tile_picked_sidegate_silu_l_kernel(tc, xT, side, w1_words, w1_scales, offs, 
 
         nc.vector.memset(w_scales[:].bitcast(I32), 0)
         for q in range(4):
-            nc.sync.dma_start(out=w_scales[32 * q : 32 * q + 4, :].bitcast(I32),
+            nc.scalar.dma_start(out=w_scales[32 * q : 32 * q + 4, :].bitcast(I32),
                                 in_=w1_scales[0, 4 * q : 4 * q + 4, :].bitcast(I32))
 
         def entries(h):

@@ -38,7 +38,8 @@ def tile_picked_sidegate_silu_l_kernel(tc, xT, side, w1_words, w1_scales, offs, 
         x_rows = xT.rearrange("(p t) w -> p t w", t=PACK)
         nc.sync.dma_start(out=planes[0][:], in_=x_rows[:, 0, :])
         nc.sync.dma_start(offsets[:], offs)
-        for t in range(1, PACK):
+        nc.scalar.dma_start(out=planes[1][:], in_=x_rows[:, 1, :])
+        for t in range(2, PACK):
             nc.sync.dma_start(out=planes[t][:], in_=x_rows[:, t, :])
         nc.sync.dma_start(out=side_rows[:], in_=side)
         nc.sync.dma_start(out=w_codes[:].bitcast(I32), in_=w1_words[0].rearrange("p n t -> p (n t)").bitcast(I32))

@@ -71,8 +71,12 @@ def tile_picked_sidegate_silu_l_kernel(tc, xT, side, w1_words, w1_scales, offs, 
             products.append(y)
 
         picked = [held.tile([P, HALF], F32, name=f"picked{h}") for h in halves]
-        for h in halves:
-            nc.vector.tensor_copy(picked[h][:], side_rows[:].indirect(entries(h)))
+        ones = held.tile([P, PIECE], F32, name="ones")
+        nc.vector.memset(ones[:], 1.0)
+        nc.vector.tensor_copy(picked[0][:], side_rows[:].indirect(entries(0)))
+        for c0 in range(0, HALF, PIECE):
+            piece = offsets[:, (HALF + c0) // LIST_ROWS : (HALF + c0 + PIECE) // LIST_ROWS]
+            nc.vector.tensor_tensor(picked[1][:, c0 : c0 + PIECE], side_rows[:].indirect(piece), ones[:], MULT)
         for i in range(S // PIECE):
             h, c0 = divmod(i * PIECE, HALF)
             gate = held.tile([P, PIECE], F32, name=f"gate{i}")

@@ -18,8 +18,9 @@ MULT = mybir.AluOpType.mult
 P = 128
 PACK = 4
 HALF = 512
-PIECE = 256
+QUARTER = 256
 LIST_ROWS = 16
+VECTOR_QUARTER = 2
 
 
 def tile_picked_sidegate_silu_l_kernel(tc, xT, side, w1_words, w1_scales, offs, out):
@@ -49,38 +50,57 @@ def tile_picked_sidegate_silu_l_kernel(tc, xT, side, w1_words, w1_scales, offs, 
             nc.scalar.dma_start(out=w_scales[32 * q : 32 * q + 4, :].bitcast(I32),
                                 in_=w1_scales[0, 4 * q : 4 * q + 4, :].bitcast(I32))
 
-        def entries(h):
-            return offsets[:, h * HALF // LIST_ROWS : (h + 1) * HALF // LIST_ROWS]
+        def entries(first, count):
+            return offsets[:, first // LIST_ROWS : (first + count) // LIST_ROWS]
 
         grouped = [held.tile([P, HALF, PACK], BF16, name=f"grouped{h}", align_bytes=64) for h in halves]
-        for t in range(PACK):
+        ones = held.tile([P, QUARTER], F32, name="ones")
+        nc.vector.memset(ones[:], 1.0)
+
+        def gather_quarter(values, table, first):
+            nc.vector.tensor_tensor(values, table[:].indirect(entries(first, QUARTER)), ones[:], MULT)
+
+        for t in range(2):
             dense = held.tile([P, HALF], F32, name=f"dense{t}")
-            nc.vector.tensor_copy(dense[:], planes[t][:].indirect(entries(0)))
+            nc.vector.tensor_copy(dense[:], planes[t][:].indirect(entries(0, HALF)))
             nc.scalar.copy(grouped[0][:, :, t], dense[:])
-            nc.vector.tensor_copy(grouped[1][:, :, t], planes[t][:].indirect(entries(1)))
+            nc.vector.tensor_copy(grouped[1][:, :, t], planes[t][:].indirect(entries(HALF, HALF)))
+
+        for t in range(2, PACK):
+            quarters = []
+            for i in range(S // QUARTER):
+                values = held.tile([P, QUARTER], F32, name=f"values{t}_{i}")
+                gather_quarter(values[:], planes[t], i * QUARTER)
+                h, c0 = divmod(i * QUARTER, HALF)
+                quarters.append((values, grouped[h][:, c0 : c0 + QUARTER, t]))
+            for i, (values, place) in enumerate(quarters):
+                if i != VECTOR_QUARTER:
+                    nc.scalar.copy(place, values[:])
+            values, place = quarters[VECTOR_QUARTER]
+            nc.vector.tensor_copy(place, values[:])
 
         products = []
         for h in halves:
             codes = held.tile([P, HALF], U32, name=f"codes{h}", align_bytes=64)
             scales = held.tile([P, HALF], U8, name=f"scales{h}", align_bytes=64)
-            nc.vector.quantize_mx(out=codes[:].bitcast(FP8X4), scales=scales[:],
-                                  in_=grouped[h][:].rearrange("p n t -> p (n t)"))
+            width = HALF if h == 0 else QUARTER
+            for c0 in range(0, HALF, width):
+                nc.vector.quantize_mx(out=codes[:, c0 : c0 + width].bitcast(FP8X4), scales=scales[:, c0 : c0 + width],
+                                      in_=grouped[h][:, c0 : c0 + width, :].rearrange("p n t -> p (n t)"))
             y = psum.tile([N, HALF], F32, name=f"y{h}")
             nc.tensor.matmul_mx(out=y[:], lhsT=w_codes[:].bitcast(FP8X4), lhsT_scale=w_scales[:],
                                 rhs=codes[:].bitcast(FP8X4), rhs_scale=scales[:], start=True, stop=True)
             products.append(y)
 
         picked = [held.tile([P, HALF], F32, name=f"picked{h}") for h in halves]
-        ones = held.tile([P, PIECE], F32, name="ones")
-        nc.vector.memset(ones[:], 1.0)
-        nc.vector.tensor_copy(picked[0][:], side_rows[:].indirect(entries(0)))
-        for c0 in range(0, HALF, PIECE):
-            piece = offsets[:, (HALF + c0) // LIST_ROWS : (HALF + c0 + PIECE) // LIST_ROWS]
-            nc.vector.tensor_tensor(picked[1][:, c0 : c0 + PIECE], side_rows[:].indirect(piece), ones[:], MULT)
-        for i in range(S // PIECE):
-            h, c0 = divmod(i * PIECE, HALF)
-            gate = held.tile([P, PIECE], F32, name=f"gate{i}")
-            nc.scalar.activation(gate[:], picked[h][:, c0 : c0 + PIECE], SILU)
-            result = held.tile([P, PIECE], F32, name=f"result{i}")
-            nc.vector.tensor_tensor(result[:], products[h][:, c0 : c0 + PIECE], gate[:], MULT)
-            nc.sync.dma_start(out=out[:, i * PIECE : (i + 1) * PIECE], in_=result[:])
+        nc.vector.tensor_copy(picked[0][:], side_rows[:].indirect(entries(0, HALF)))
+        for c0 in range(0, HALF, QUARTER):
+            gather_quarter(picked[1][:, c0 : c0 + QUARTER], side_rows, HALF + c0)
+
+        for i in range(S // QUARTER):
+            h, c0 = divmod(i * QUARTER, HALF)
+            gate = held.tile([P, QUARTER], F32, name=f"gate{i}")
+            nc.scalar.activation(gate[:], picked[h][:, c0 : c0 + QUARTER], SILU)
+            result = held.tile([P, QUARTER], F32, name=f"result{i}")
+            nc.vector.tensor_tensor(result[:], products[h][:, c0 : c0 + QUARTER], gate[:], MULT)
+            nc.sync.dma_start(out=out[:, i * QUARTER : (i + 1) * QUARTER], in_=result[:])

@@ -19,6 +19,7 @@ P = 128
 PACK = 4
 HALF = 512
 QUARTER = 256
+EIGHTH = 128
 LIST_ROWS = 16
 VECTOR_QUARTER = 2
 
@@ -54,11 +55,11 @@ def tile_picked_sidegate_silu_l_kernel(tc, xT, side, w1_words, w1_scales, offs, 
             return offsets[:, first // LIST_ROWS : (first + count) // LIST_ROWS]
 
         grouped = [held.tile([P, HALF, PACK], BF16, name=f"grouped{h}", align_bytes=64) for h in halves]
-        ones = held.tile([P, QUARTER], F32, name="ones")
+        ones = held.tile([P, HALF], F32, name="ones")
         nc.vector.memset(ones[:], 1.0)
 
-        def gather_quarter(values, table, first):
-            nc.vector.tensor_tensor(values, table[:].indirect(entries(first, QUARTER)), ones[:], MULT)
+        def gather_piece(values, table, first, count):
+            nc.vector.tensor_tensor(values, table[:].indirect(entries(first, count)), ones[:, :count], MULT)
 
         for t in range(2):
             dense = held.tile([P, HALF], F32, name=f"dense{t}")
@@ -70,7 +71,7 @@ def tile_picked_sidegate_silu_l_kernel(tc, xT, side, w1_words, w1_scales, offs, 
             quarters = []
             for i in range(S // QUARTER):
                 values = held.tile([P, QUARTER], F32, name=f"values{t}_{i}")
-                gather_quarter(values[:], planes[t], i * QUARTER)
+                gather_piece(values[:], planes[t], i * QUARTER, QUARTER)
                 h, c0 = divmod(i * QUARTER, HALF)
                 quarters.append((values, grouped[h][:, c0 : c0 + QUARTER, t]))
             for i, (values, place) in enumerate(quarters):
@@ -92,15 +93,36 @@ def tile_picked_sidegate_silu_l_kernel(tc, xT, side, w1_words, w1_scales, offs, 
                                 rhs=codes[:].bitcast(FP8X4), rhs_scale=scales[:], start=True, stop=True)
             products.append(y)
 
-        picked = [held.tile([P, HALF], F32, name=f"picked{h}") for h in halves]
-        nc.vector.tensor_copy(picked[0][:], side_rows[:].indirect(entries(0, HALF)))
-        for c0 in range(0, HALF, QUARTER):
-            gather_quarter(picked[1][:, c0 : c0 + QUARTER], side_rows, HALF + c0)
+        picked = held.tile([P, S - EIGHTH], F32, name="picked")
+        gates = held.tile([P, S], F32, name="gates")
+        results = held.tile([P, S], F32, name="results")
 
-        for i in range(S // QUARTER):
-            h, c0 = divmod(i * QUARTER, HALF)
-            gate = held.tile([P, QUARTER], F32, name=f"gate{i}")
-            nc.scalar.activation(gate[:], picked[h][:, c0 : c0 + QUARTER], SILU)
-            result = held.tile([P, QUARTER], F32, name=f"result{i}")
-            nc.vector.tensor_tensor(result[:], products[h][:, c0 : c0 + QUARTER], gate[:], MULT)
-            nc.sync.dma_start(out=out[:, i * QUARTER : (i + 1) * QUARTER], in_=result[:])
+        def silu(first, count, values):
+            nc.scalar.activation(gates[:, first : first + count], values, SILU)
+
+        def multiply(first, count):
+            h, c0 = divmod(first, HALF)
+            nc.vector.tensor_tensor(results[:, first : first + count], products[h][:, c0 : c0 + count],
+                                    gates[:, first : first + count], MULT)
+
+        def store(first):
+            nc.sync.dma_start(out=out[:, first : first + QUARTER], in_=results[:, first : first + QUARTER])
+
+        last = S - EIGHTH
+        gather_piece(picked[:, :QUARTER], side_rows, 0, QUARTER)
+        gather_piece(picked[:, QUARTER:HALF], side_rows, QUARTER, QUARTER)
+        gather_piece(picked[:, HALF:last], side_rows, HALF, last - HALF)
+        silu(0, QUARTER, picked[:, :QUARTER])
+        silu(QUARTER, QUARTER, picked[:, QUARTER:HALF])
+        multiply(0, QUARTER)
+        store(0)
+        gather_piece(picked[:, QUARTER : QUARTER + EIGHTH], side_rows, last, EIGHTH)
+        silu(HALF, QUARTER, picked[:, HALF : HALF + QUARTER])
+        silu(HALF + QUARTER, EIGHTH, picked[:, HALF + QUARTER : last])
+        silu(last, EIGHTH, picked[:, QUARTER : QUARTER + EIGHTH])
+        for first in (QUARTER, HALF):
+            multiply(first, QUARTER)
+            store(first)
+        multiply(HALF + QUARTER, EIGHTH)
+        multiply(last, EIGHTH)
+        store(HALF + QUARTER)

@@ -55,7 +55,7 @@ def tile_picked_sidegate_silu_l_kernel(tc, xT, side, w1_words, w1_scales, offs, 
             return offsets[:, first // LIST_ROWS : (first + count) // LIST_ROWS]
 
         grouped = [held.tile([P, HALF, PACK], BF16, name=f"grouped{h}", align_bytes=64) for h in halves]
-        ones = held.tile([P, HALF], F32, name="ones")
+        ones = held.tile([P, QUARTER + EIGHTH], F32, name="ones")
         nc.vector.memset(ones[:], 1.0)
 
         def gather_piece(values, table, first, count):
@@ -116,10 +116,13 @@ def tile_picked_sidegate_silu_l_kernel(tc, xT, side, w1_words, w1_scales, offs, 
         silu(QUARTER, QUARTER, picked[:, QUARTER:HALF])
         multiply(0, QUARTER)
         store(0)
-        gather_piece(picked[:, QUARTER : QUARTER + EIGHTH], side_rows, last, EIGHTH)
+
+        picked_last = picked[:, QUARTER : QUARTER + EIGHTH]
+        gather_piece(picked_last, side_rows, last, EIGHTH)
         silu(HALF, QUARTER, picked[:, HALF : HALF + QUARTER])
         silu(HALF + QUARTER, EIGHTH, picked[:, HALF + QUARTER : last])
-        silu(last, EIGHTH, picked[:, QUARTER : QUARTER + EIGHTH])
+        silu(last, EIGHTH, picked_last)
+
         for first in (QUARTER, HALF):
             multiply(first, QUARTER)
             store(first)

@@ -105,8 +105,8 @@ def tile_picked_sidegate_silu_l_kernel(tc, xT, side, w1_words, w1_scales, offs, 
             nc.vector.tensor_tensor(results[:, first : first + count], products[h][:, c0 : c0 + count],
                                     gates[:, first : first + count], MULT)
 
-        def store(first):
-            nc.sync.dma_start(out=out[:, first : first + QUARTER], in_=results[:, first : first + QUARTER])
+        def store(first, queue=nc.sync):
+            queue.dma_start(out=out[:, first : first + QUARTER], in_=results[:, first : first + QUARTER])
 
         last = S - EIGHTH
         gather_piece(picked[:, :QUARTER], side_rows, 0, QUARTER)
@@ -123,9 +123,9 @@ def tile_picked_sidegate_silu_l_kernel(tc, xT, side, w1_words, w1_scales, offs, 
         silu(HALF + QUARTER, EIGHTH, picked[:, HALF + QUARTER : last])
         silu(last, EIGHTH, picked_last)
 
-        for first in (QUARTER, HALF):
+        for first, queue in ((QUARTER, nc.sync), (HALF, nc.scalar)):
             multiply(first, QUARTER)
-            store(first)
+            store(first, queue)
         multiply(HALF + QUARTER, EIGHTH)
         multiply(last, EIGHTH)
         store(HALF + QUARTER)

@@ -105,8 +105,8 @@ def tile_picked_sidegate_silu_l_kernel(tc, xT, side, w1_words, w1_scales, offs, 
             nc.vector.tensor_tensor(results[:, first : first + count], products[h][:, c0 : c0 + count],
                                     gates[:, first : first + count], MULT)
 
-        def store(first, queue=nc.sync):
-            queue.dma_start(out=out[:, first : first + QUARTER], in_=results[:, first : first + QUARTER])
+        def store(first, count=QUARTER, queue=nc.sync):
+            queue.dma_start(out=out[:, first : first + count], in_=results[:, first : first + count])
 
         last = S - EIGHTH
         gather_piece(picked[:, :QUARTER], side_rows, 0, QUARTER)
@@ -125,7 +125,7 @@ def tile_picked_sidegate_silu_l_kernel(tc, xT, side, w1_words, w1_scales, offs, 
 
         for first, queue in ((QUARTER, nc.sync), (HALF, nc.scalar)):
             multiply(first, QUARTER)
-            store(first, queue)
-        multiply(HALF + QUARTER, EIGHTH)
-        multiply(last, EIGHTH)
-        store(HALF + QUARTER)
+            store(first, queue=queue)
+        for first in (HALF + QUARTER, last):
+            multiply(first, EIGHTH)
+            store(first, EIGHTH)

@@ -109,23 +109,26 @@ def tile_picked_sidegate_silu_l_kernel(tc, xT, side, w1_words, w1_scales, offs, 
             queue.dma_start(out=out[:, first : first + count], in_=results[:, first : first + count])
 
         last = S - EIGHTH
+        early = QUARTER + EIGHTH
         gather_piece(picked[:, :QUARTER], side_rows, 0, QUARTER)
         gather_piece(picked[:, QUARTER:HALF], side_rows, QUARTER, QUARTER)
         gather_piece(picked[:, HALF:last], side_rows, HALF, last - HALF)
         silu(0, QUARTER, picked[:, :QUARTER])
         silu(QUARTER, QUARTER, picked[:, QUARTER:HALF])
-        multiply(0, QUARTER)
-        store(0)
+        for first, count in ((0, QUARTER), (QUARTER, EIGHTH)):
+            multiply(first, count)
+            store(first, count)
 
         picked_last = picked[:, QUARTER : QUARTER + EIGHTH]
         gather_piece(picked_last, side_rows, last, EIGHTH)
-        silu(HALF, QUARTER, picked[:, HALF : HALF + QUARTER])
-        silu(HALF + QUARTER, EIGHTH, picked[:, HALF + QUARTER : last])
+        silu(HALF, EIGHTH, picked[:, HALF : HALF + EIGHTH])
+        silu(HALF + EIGHTH, QUARTER, picked[:, HALF + EIGHTH : last])
         silu(last, EIGHTH, picked_last)
 
-        for first, queue in ((QUARTER, nc.sync), (HALF, nc.scalar)):
-            multiply(first, QUARTER)
-            store(first, queue=queue)
-        for first in (HALF + QUARTER, last):
-            multiply(first, EIGHTH)
-            store(first, EIGHTH)
+        multiply(early, EIGHTH)
+        multiply(HALF, EIGHTH)
+        store(early)
+        multiply(HALF + EIGHTH, QUARTER)
+        store(HALF + EIGHTH, queue=nc.scalar)
+        multiply(last, EIGHTH)
+        store(last, EIGHTH)

@@ -13,20 +13,19 @@ U16 = mybir.dt.uint16
 U8 = mybir.dt.uint8
 FP8X4 = mybir.dt.float8_e4m3fn_x4
 SILU = mybir.ActivationFunctionType.Silu
+COPY = mybir.ActivationFunctionType.Copy
 MULT = mybir.AluOpType.mult
 
 P = 128
 PACK = 4
-HALF = 512
 QUARTER = 256
 EIGHTH = 128
 LIST_ROWS = 16
-VECTOR_QUARTER = 2
 
 
 def tile_picked_sidegate_silu_l_kernel(tc, xT, side, w1_words, w1_scales, offs, out):
     nc = tc.nc
-    halves = range(S // HALF)
+    quarters = range(S // QUARTER)
     with ExitStack() as ctx:
         held = ctx.enter_context(tc.tile_pool(name="held", bufs=1))
         psum = ctx.enter_context(tc.psum_pool(name="psum", bufs=1))
@@ -51,84 +50,81 @@ def tile_picked_sidegate_silu_l_kernel(tc, xT, side, w1_words, w1_scales, offs, 
             nc.scalar.dma_start(out=w_scales[32 * q : 32 * q + 4, :].bitcast(I32),
                                 in_=w1_scales[0, 4 * q : 4 * q + 4, :].bitcast(I32))
 
+        ones = held.tile([P, EIGHTH], F32, name="ones")
+        nc.vector.memset(ones[:], 1.0)
+
+        warm = held.tile([P, 1], F32, name="warm")
+        nc.scalar.activation(warm[:], ones[:, :1], SILU)
+
         def entries(first, count):
             return offsets[:, first // LIST_ROWS : (first + count) // LIST_ROWS]
 
-        grouped = [held.tile([P, HALF, PACK], BF16, name=f"grouped{h}", align_bytes=64) for h in halves]
-        ones = held.tile([P, QUARTER + EIGHTH], F32, name="ones")
-        nc.vector.memset(ones[:], 1.0)
+        grouped = [held.tile([P, QUARTER, PACK], BF16, name=f"grouped{i}", align_bytes=64) for i in quarters]
+        codes = held.tile([P, S], U32, name="codes", align_bytes=64)
+        scales = held.tile([P, S], U8, name="scales", align_bytes=64)
 
-        def gather_piece(values, table, first, count):
-            nc.vector.tensor_tensor(values, table[:].indirect(entries(first, count)), ones[:, :count], MULT)
+        def quantize(i):
+            cols = slice(i * QUARTER, (i + 1) * QUARTER)
+            nc.vector.quantize_mx(out=codes[:, cols].bitcast(FP8X4), scales=scales[:, cols],
+                                  in_=grouped[i][:].rearrange("p n t -> p (n t)"))
 
-        for t in range(2):
-            dense = held.tile([P, HALF], F32, name=f"dense{t}")
-            nc.vector.tensor_copy(dense[:], planes[t][:].indirect(entries(0, HALF)))
-            nc.scalar.copy(grouped[0][:, :, t], dense[:])
-            nc.vector.tensor_copy(grouped[1][:, :, t], planes[t][:].indirect(entries(HALF, HALF)))
+        for t in range(PACK):
+            dense = [held.tile([P, QUARTER], BF16, name=f"dense{t}_{i}") for i in quarters]
+            for i in quarters[:-1]:
+                nc.scalar.activation(dense[i][:], planes[t][:].indirect(entries(i * QUARTER, QUARTER)), COPY)
+            nc.vector.tensor_copy(dense[-1][:], planes[t][:].indirect(entries(S - QUARTER, QUARTER)))
+            order = (0, 3, 1, 2)
+            for step, i in enumerate(order):
+                nc.vector.tensor_copy(grouped[i][:, :, t], dense[i][:])
+                if t == PACK - 1 and step > 0:
+                    quantize(order[step - 1])
+        quantize(order[-1])
 
-        for t in range(2, PACK):
-            quarters = []
-            for i in range(S // QUARTER):
-                values = held.tile([P, QUARTER], F32, name=f"values{t}_{i}")
-                gather_piece(values[:], planes[t], i * QUARTER, QUARTER)
-                h, c0 = divmod(i * QUARTER, HALF)
-                quarters.append((values, grouped[h][:, c0 : c0 + QUARTER, t]))
-            for i, (values, place) in enumerate(quarters):
-                if i != VECTOR_QUARTER:
-                    nc.scalar.copy(place, values[:])
-            values, place = quarters[VECTOR_QUARTER]
-            nc.vector.tensor_copy(place, values[:])
-
-        products = []
-        for h in halves:
-            codes = held.tile([P, HALF], U32, name=f"codes{h}", align_bytes=64)
-            scales = held.tile([P, HALF], U8, name=f"scales{h}", align_bytes=64)
-            width = HALF if h == 0 else QUARTER
-            for c0 in range(0, HALF, width):
-                nc.vector.quantize_mx(out=codes[:, c0 : c0 + width].bitcast(FP8X4), scales=scales[:, c0 : c0 + width],
-                                      in_=grouped[h][:, c0 : c0 + width, :].rearrange("p n t -> p (n t)"))
-            y = psum.tile([N, HALF], F32, name=f"y{h}")
+        b1, a1, b2, b3, a2 = (0, 128), (128, 256), (384, 256), (640, 256), (896, 128)
+        products = {}
+        for first, count in (b1, a1, b2, b3, a2):
+            y = psum.tile([N, count], F32, name=f"y{first}")
             nc.tensor.matmul_mx(out=y[:], lhsT=w_codes[:].bitcast(FP8X4), lhsT_scale=w_scales[:],
-                                rhs=codes[:].bitcast(FP8X4), rhs_scale=scales[:], start=True, stop=True)
-            products.append(y)
+                                rhs=codes[:, first : first + count].bitcast(FP8X4),
+                                rhs_scale=scales[:, first : first + count], start=True, stop=True)
+            products[first] = y
 
-        picked = held.tile([P, S - EIGHTH], F32, name="picked")
+        picked = held.tile([P, S], F32, name="picked")
         gates = held.tile([P, S], F32, name="gates")
         results = held.tile([P, S], F32, name="results")
 
-        def silu(first, count, values):
-            nc.scalar.activation(gates[:, first : first + count], values, SILU)
+        def cols(tile, piece):
+            return tile[:, piece[0] : piece[0] + piece[1]]
 
-        def multiply(first, count):
-            h, c0 = divmod(first, HALF)
-            nc.vector.tensor_tensor(results[:, first : first + count], products[h][:, c0 : c0 + count],
-                                    gates[:, first : first + count], MULT)
+        def gather_vector(piece):
+            window = side_rows[:].indirect(entries(*piece))
+            if piece[1] == EIGHTH:
+                nc.vector.tensor_tensor(cols(picked, piece), window, ones[:], MULT)
+            else:
+                nc.vector.tensor_copy(cols(picked, piece), window)
 
-        def store(first, count=QUARTER, queue=nc.sync):
-            queue.dma_start(out=out[:, first : first + count], in_=results[:, first : first + count])
+        def gather_scalar(piece):
+            nc.scalar.activation(cols(picked, piece), side_rows[:].indirect(entries(*piece)), COPY)
 
-        last = S - EIGHTH
-        early = QUARTER + EIGHTH
-        gather_piece(picked[:, :QUARTER], side_rows, 0, QUARTER)
-        gather_piece(picked[:, QUARTER:HALF], side_rows, QUARTER, QUARTER)
-        gather_piece(picked[:, HALF:last], side_rows, HALF, last - HALF)
-        silu(0, QUARTER, picked[:, :QUARTER])
-        silu(QUARTER, QUARTER, picked[:, QUARTER:HALF])
-        for first, count in ((0, QUARTER), (QUARTER, EIGHTH)):
-            multiply(first, count)
-            store(first, count)
+        def silu(piece):
+            nc.scalar.activation(cols(gates, piece), cols(picked, piece), SILU)
 
-        picked_last = picked[:, QUARTER : QUARTER + EIGHTH]
-        gather_piece(picked_last, side_rows, last, EIGHTH)
-        silu(HALF, EIGHTH, picked[:, HALF : HALF + EIGHTH])
-        silu(HALF + EIGHTH, QUARTER, picked[:, HALF + EIGHTH : last])
-        silu(last, EIGHTH, picked_last)
+        def finish(piece):
+            nc.vector.tensor_tensor(cols(results, piece), products[piece[0]][:], cols(gates, piece), MULT)
+            nc.sync.dma_start(out=cols(out, piece), in_=cols(results, piece))
 
-        multiply(early, EIGHTH)
-        multiply(HALF, EIGHTH)
-        store(early)
-        multiply(HALF + EIGHTH, QUARTER)
-        store(HALF + EIGHTH, queue=nc.scalar)
-        multiply(last, EIGHTH)
-        store(last, EIGHTH)
+        gather_vector(b1)
+        gather_scalar(a1)
+        gather_vector(b2)
+        silu(b1)
+        silu(a1)
+        finish(b1)
+        gather_vector(b3)
+        silu(b2)
+        gather_scalar(a2)
+        finish(a1)
+        finish(b2)
+        silu(b3)
+        silu(a2)
+        finish(b3)
+        finish(a2)

@@ -18,6 +18,8 @@ MULT = mybir.AluOpType.mult
 
 P = 128
 PACK = 4
+SYNC_SHARE = 6080
+HALF = 512
 QUARTER = 256
 EIGHTH = 128
 LIST_ROWS = 16
@@ -31,17 +33,17 @@ def tile_picked_sidegate_silu_l_kernel(tc, xT, side, w1_words, w1_scales, offs, 
         psum = ctx.enter_context(tc.psum_pool(name="psum", bufs=1))
 
         offsets = held.tile([P, S // LIST_ROWS], U16, name="offsets")
-        planes = [held.tile([P, T], F32, name=f"plane{t}") for t in range(PACK)]
+        early = held.tile([P, (PACK - 1) * T], F32, name="early")
+        last_plane = held.tile([P, T], F32, name="last_plane")
         side_rows = held.tile([P, T], F32, name="side_rows")
         w_codes = held.tile([P, N], U32, name="w_codes", align_bytes=64)
         w_scales = held.tile([P, N], U8, name="w_scales", align_bytes=64)
 
-        x_rows = xT.rearrange("(p t) w -> p t w", t=PACK)
-        nc.sync.dma_start(out=planes[0][:], in_=x_rows[:, 0, :])
+        x_rows = xT.rearrange("(p t) w -> p (t w)", t=PACK)
+        nc.sync.dma_start(out=early[:, :SYNC_SHARE], in_=x_rows[:, :SYNC_SHARE])
         nc.sync.dma_start(offsets[:], offs)
-        nc.scalar.dma_start(out=planes[1][:], in_=x_rows[:, 1, :])
-        for t in range(2, PACK):
-            nc.sync.dma_start(out=planes[t][:], in_=x_rows[:, t, :])
+        nc.scalar.dma_start(out=early[:, SYNC_SHARE:], in_=x_rows[:, SYNC_SHARE : (PACK - 1) * T])
+        nc.sync.dma_start(out=last_plane[:], in_=x_rows[:, (PACK - 1) * T :])
         nc.sync.dma_start(out=side_rows[:], in_=side)
         nc.sync.dma_start(out=w_codes[:].bitcast(I32), in_=w1_words[0].rearrange("p n t -> p (n t)").bitcast(I32))
 
@@ -68,16 +70,32 @@ def tile_picked_sidegate_silu_l_kernel(tc, xT, side, w1_words, w1_scales, offs, 
             nc.vector.quantize_mx(out=codes[:, cols].bitcast(FP8X4), scales=scales[:, cols],
                                   in_=grouped[i][:].rearrange("p n t -> p (n t)"))
 
-        for t in range(PACK):
-            dense = [held.tile([P, QUARTER], BF16, name=f"dense{t}_{i}") for i in quarters]
-            for i in quarters[:-1]:
-                nc.scalar.activation(dense[i][:], planes[t][:].indirect(entries(i * QUARTER, QUARTER)), COPY)
-            nc.vector.tensor_copy(dense[-1][:], planes[t][:].indirect(entries(S - QUARTER, QUARTER)))
-            order = (0, 3, 1, 2)
-            for step, i in enumerate(order):
-                nc.vector.tensor_copy(grouped[i][:, :, t], dense[i][:])
-                if t == PACK - 1 and step > 0:
-                    quantize(order[step - 1])
+        def weave(i, pair, values):
+            nc.vector.tensor_copy(grouped[i][:, :, 2 * pair : 2 * pair + 2], values.rearrange("p t n -> p n t"))
+
+        low = [held.tile([P, 2, HALF], F32, name=f"low{h}") for h in range(S // HALF)]
+        high = [held.tile([P, 2, HALF], F32, name=f"high{h}") for h in range(S // HALF)]
+        for t in range(2):
+            window = early[:, t * T : (t + 1) * T]
+            nc.scalar.activation(low[0][:, t, :], window.indirect(entries(0, HALF)), COPY)
+            nc.vector.tensor_copy(low[1][:, t, :], window.indirect(entries(HALF, HALF)))
+        for h in range(S // HALF):
+            nc.scalar.activation(high[h][:, 0, :], early[:, 2 * T :].indirect(entries(h * HALF, HALF)), COPY)
+
+        def quarter(tiles, i):
+            h, c0 = divmod(i * QUARTER, HALF)
+            return tiles[h][:, :, c0 : c0 + QUARTER]
+
+        for i in reversed(quarters):
+            weave(i, 0, quarter(low, i))
+        for i in quarters[:-1]:
+            nc.scalar.activation(quarter(high, i)[:, 1, :], last_plane[:].indirect(entries(i * QUARTER, QUARTER)), COPY)
+        nc.vector.tensor_copy(quarter(high, 3)[:, 1, :], last_plane[:].indirect(entries(S - QUARTER, QUARTER)))
+        order = (3, 0, 1, 2)
+        for step, i in enumerate(order):
+            weave(i, 1, quarter(high, i))
+            if step > 0:
+                quantize(order[step - 1])
         quantize(order[-1])
 
         b1, a1, b2, b3, a2 = (0, 128), (128, 256), (384, 256), (640, 256), (896, 128)

@@ -49,8 +49,8 @@ def tile_picked_sidegate_silu_l_kernel(tc, xT, side, w1_words, w1_scales, offs, 
 
         nc.vector.memset(w_scales[:].bitcast(I32), 0)
         for q in range(4):
-            nc.scalar.dma_start(out=w_scales[32 * q : 32 * q + 4, :].bitcast(I32),
-                                in_=w1_scales[0, 4 * q : 4 * q + 4, :].bitcast(I32))
+            nc.sync.dma_start(out=w_scales[32 * q : 32 * q + 4, :].bitcast(I32),
+                              in_=w1_scales[0, 4 * q : 4 * q + 4, :].bitcast(I32))
 
         ones = held.tile([P, EIGHTH], F32, name="ones")
         nc.vector.memset(ones[:], 1.0)

@@ -49,8 +49,8 @@ def tile_picked_sidegate_silu_l_kernel(tc, xT, side, w1_words, w1_scales, offs, 
 
         nc.vector.memset(w_scales[:].bitcast(I32), 0)
         for q in range(4):
-            nc.sync.dma_start(out=w_scales[32 * q : 32 * q + 4, :].bitcast(I32),
-                              in_=w1_scales[0, 4 * q : 4 * q + 4, :].bitcast(I32))
+            nc.scalar.dma_start(out=w_scales[32 * q : 32 * q + 4, :].bitcast(I32),
+                                in_=w1_scales[0, 4 * q : 4 * q + 4, :].bitcast(I32))
 
         ones = held.tile([P, EIGHTH], F32, name="ones")
         nc.vector.memset(ones[:], 1.0)
@@ -98,9 +98,9 @@ def tile_picked_sidegate_silu_l_kernel(tc, xT, side, w1_words, w1_scales, offs, 
                 quantize(order[step - 1])
         quantize(order[-1])
 
-        b1, a1, b2, b3, a2 = (0, 128), (128, 256), (384, 256), (640, 256), (896, 128)
+        pieces = ((0, 128), (128, 256), (384, 256), (640, 128), (768, 256))
         products = {}
-        for first, count in (b1, a1, b2, b3, a2):
+        for first, count in pieces:
             y = psum.tile([N, count], F32, name=f"y{first}")
             nc.tensor.matmul_mx(out=y[:], lhsT=w_codes[:].bitcast(FP8X4), lhsT_scale=w_scales[:],
                                 rhs=codes[:, first : first + count].bitcast(FP8X4),
@@ -111,38 +111,26 @@ def tile_picked_sidegate_silu_l_kernel(tc, xT, side, w1_words, w1_scales, offs, 
         gates = held.tile([P, S], F32, name="gates")
         results = held.tile([P, S], F32, name="results")
 
-        def cols(tile, piece):
-            return tile[:, piece[0] : piece[0] + piece[1]]
+        def cols(tile, first, count):
+            return tile[:, first : first + count]
 
-        def gather_vector(piece):
-            window = side_rows[:].indirect(entries(*piece))
-            if piece[1] == EIGHTH:
-                nc.vector.tensor_tensor(cols(picked, piece), window, ones[:], MULT)
+        for i, (first, count) in enumerate(pieces):
+            window = side_rows[:].indirect(entries(first, count))
+            if i % 2:
+                nc.scalar.activation(cols(picked, first, count), window, COPY)
+            elif count == EIGHTH:
+                nc.vector.tensor_tensor(cols(picked, first, count), window, ones[:], MULT)
             else:
-                nc.vector.tensor_copy(cols(picked, piece), window)
+                nc.vector.tensor_copy(cols(picked, first, count), window)
 
-        def gather_scalar(piece):
-            nc.scalar.activation(cols(picked, piece), side_rows[:].indirect(entries(*piece)), COPY)
-
-        def silu(piece):
-            nc.scalar.activation(cols(gates, piece), cols(picked, piece), SILU)
-
-        def finish(piece):
-            nc.vector.tensor_tensor(cols(results, piece), products[piece[0]][:], cols(gates, piece), MULT)
-            nc.sync.dma_start(out=cols(out, piece), in_=cols(results, piece))
-
-        gather_vector(b1)
-        gather_scalar(a1)
-        gather_vector(b2)
-        silu(b1)
-        silu(a1)
-        finish(b1)
-        gather_vector(b3)
-        silu(b2)
-        gather_scalar(a2)
-        finish(a1)
-        finish(b2)
-        silu(b3)
-        silu(a2)
-        finish(b3)
-        finish(a2)
+        steps = pieces[:-1] + ((768, 128), (896, 128))
+        stores = ((0, 128), (128, 256), (384, 256), (640, 256), (896, 128))
+        for first, count in steps:
+            nc.scalar.activation(cols(gates, first, count), cols(picked, first, count), SILU)
+        for first, count in steps:
+            bank = max(start for start in products if start <= first)
+            nc.vector.tensor_tensor(cols(results, first, count), cols(products[bank], first - bank, count),
+                                    cols(gates, first, count), MULT)
+            for start, width in stores:
+                if start + width == first + count:
+                    nc.sync.dma_start(out=cols(out, start, width), in_=cols(results, start, width))

@@ -98,14 +98,13 @@ def tile_picked_sidegate_silu_l_kernel(tc, xT, side, w1_words, w1_scales, offs, 
                 quantize(order[step - 1])
         quantize(order[-1])
 
-        pieces = ((0, 128), (128, 256), (384, 256), (640, 128), (768, 256))
-        products = {}
-        for first, count in pieces:
-            y = psum.tile([N, count], F32, name=f"y{first}")
+        products = []
+        for i in quarters:
+            y = psum.tile([N, QUARTER], F32, name=f"y{i}")
             nc.tensor.matmul_mx(out=y[:], lhsT=w_codes[:].bitcast(FP8X4), lhsT_scale=w_scales[:],
-                                rhs=codes[:, first : first + count].bitcast(FP8X4),
-                                rhs_scale=scales[:, first : first + count], start=True, stop=True)
-            products[first] = y
+                                rhs=codes[:, i * QUARTER : (i + 1) * QUARTER].bitcast(FP8X4),
+                                rhs_scale=scales[:, i * QUARTER : (i + 1) * QUARTER], start=True, stop=True)
+            products.append(y)
 
         picked = held.tile([P, S], F32, name="picked")
         gates = held.tile([P, S], F32, name="gates")
@@ -114,23 +113,18 @@ def tile_picked_sidegate_silu_l_kernel(tc, xT, side, w1_words, w1_scales, offs, 
         def cols(tile, first, count):
             return tile[:, first : first + count]
 
-        for i, (first, count) in enumerate(pieces):
-            window = side_rows[:].indirect(entries(first, count))
-            if i % 2:
-                nc.scalar.activation(cols(picked, first, count), window, COPY)
-            elif count == EIGHTH:
-                nc.vector.tensor_tensor(cols(picked, first, count), window, ones[:], MULT)
-            else:
-                nc.vector.tensor_copy(cols(picked, first, count), window)
+        def side_window(first, count):
+            return side_rows[:].indirect(entries(first, count))
 
-        steps = pieces[:-1] + ((768, 128), (896, 128))
-        stores = ((0, 128), (128, 256), (384, 256), (640, 256), (896, 128))
-        for first, count in steps:
-            nc.scalar.activation(cols(gates, first, count), cols(picked, first, count), SILU)
-        for first, count in steps:
-            bank = max(start for start in products if start <= first)
-            nc.vector.tensor_tensor(cols(results, first, count), cols(products[bank], first - bank, count),
+        nc.vector.tensor_tensor(cols(picked, 0, EIGHTH), side_window(0, EIGHTH), ones[:], MULT)
+        for first, count in ((EIGHTH, EIGHTH), (QUARTER, QUARTER)):
+            nc.scalar.activation(cols(picked, first, count), side_window(first, count), COPY)
+        for i in quarters[2:]:
+            nc.vector.tensor_copy(cols(picked, i * QUARTER, QUARTER), side_window(i * QUARTER, QUARTER))
+        for i in quarters:
+            nc.scalar.activation(cols(gates, i * QUARTER, QUARTER), cols(picked, i * QUARTER, QUARTER), SILU)
+        for first, count in ((0, EIGHTH), (EIGHTH, EIGHTH)) + tuple((i * QUARTER, QUARTER) for i in quarters[1:]):
+            i, c0 = divmod(first, QUARTER)
+            nc.vector.tensor_tensor(cols(results, first, count), cols(products[i], c0, count),
                                     cols(gates, first, count), MULT)
-            for start, width in stores:
-                if start + width == first + count:
-                    nc.sync.dma_start(out=cols(out, start, width), in_=cols(results, start, width))
+            nc.sync.dma_start(out=cols(out, first, count), in_=cols(results, first, count))

@@ -127,4 +127,5 @@ def tile_picked_sidegate_silu_l_kernel(tc, xT, side, w1_words, w1_scales, offs, 
             i, c0 = divmod(first, QUARTER)
             nc.vector.tensor_tensor(cols(results, first, count), cols(products[i], c0, count),
                                     cols(gates, first, count), MULT)
-            nc.sync.dma_start(out=cols(out, first, count), in_=cols(results, first, count))
+            queue = nc.scalar if first == HALF else nc.sync
+            queue.dma_start(out=cols(out, first, count), in_=cols(results, first, count))

from contextlib import ExitStack

import concourse.mybir as mybir

K, T, S, N = 512, 4096, 1024, 128
FLOPS = 2 * K * N * S

F32 = mybir.dt.float32
BF16 = mybir.dt.bfloat16
I32 = mybir.dt.int32
U32 = mybir.dt.uint32
U16 = mybir.dt.uint16
U8 = mybir.dt.uint8
FP8X4 = mybir.dt.float8_e4m3fn_x4
SILU = mybir.ActivationFunctionType.Silu
COPY = mybir.ActivationFunctionType.Copy
MULT = mybir.AluOpType.mult

P = 128
PACK = 4
SYNC_SHARE = 6080
HALF = 512
QUARTER = 256
EIGHTH = 128
LIST_ROWS = 16


def tile_picked_sidegate_silu_l_kernel(tc, xT, side, w1_words, w1_scales, offs, out):
    nc = tc.nc
    quarters = range(S // QUARTER)
    with ExitStack() as ctx:
        held = ctx.enter_context(tc.tile_pool(name="held", bufs=1))
        psum = ctx.enter_context(tc.psum_pool(name="psum", bufs=1))

        offsets = held.tile([P, S // LIST_ROWS], U16, name="offsets")
        early = held.tile([P, (PACK - 1) * T], F32, name="early")
        last_plane = held.tile([P, T], F32, name="last_plane")
        side_rows = held.tile([P, T], F32, name="side_rows")
        w_codes = held.tile([P, N], U32, name="w_codes", align_bytes=64)
        w_scales = held.tile([P, N], U8, name="w_scales", align_bytes=64)

        x_rows = xT.rearrange("(p t) w -> p (t w)", t=PACK)
        nc.sync.dma_start(out=early[:, :SYNC_SHARE], in_=x_rows[:, :SYNC_SHARE])
        nc.sync.dma_start(offsets[:], offs)
        nc.scalar.dma_start(out=early[:, SYNC_SHARE:], in_=x_rows[:, SYNC_SHARE : (PACK - 1) * T])
        nc.sync.dma_start(out=last_plane[:], in_=x_rows[:, (PACK - 1) * T :])
        nc.sync.dma_start(out=side_rows[:], in_=side)
        nc.sync.dma_start(out=w_codes[:].bitcast(I32), in_=w1_words[0].rearrange("p n t -> p (n t)").bitcast(I32))

        nc.vector.memset(w_scales[:].bitcast(I32), 0)
        for q in range(4):
            nc.scalar.dma_start(out=w_scales[32 * q : 32 * q + 4, :].bitcast(I32),
                                in_=w1_scales[0, 4 * q : 4 * q + 4, :].bitcast(I32))

        ones = held.tile([P, EIGHTH], F32, name="ones")
        nc.vector.memset(ones[:], 1.0)

        warm = held.tile([P, 1], F32, name="warm")
        nc.scalar.activation(warm[:], ones[:, :1], SILU)

        def entries(first, count):
            return offsets[:, first // LIST_ROWS : (first + count) // LIST_ROWS]

        grouped = [held.tile([P, QUARTER, PACK], BF16, name=f"grouped{i}", align_bytes=64) for i in quarters]
        codes = held.tile([P, S], U32, name="codes", align_bytes=64)
        scales = held.tile([P, S], U8, name="scales", align_bytes=64)

        def quantize(i):
            cols = slice(i * QUARTER, (i + 1) * QUARTER)
            nc.vector.quantize_mx(out=codes[:, cols].bitcast(FP8X4), scales=scales[:, cols],
                                  in_=grouped[i][:].rearrange("p n t -> p (n t)"))

        def weave(i, pair, values):
            nc.vector.tensor_copy(grouped[i][:, :, 2 * pair : 2 * pair + 2], values.rearrange("p t n -> p n t"))

        low = [held.tile([P, 2, HALF], F32, name=f"low{h}") for h in range(S // HALF)]
        high = [held.tile([P, 2, HALF], F32, name=f"high{h}") for h in range(S // HALF)]
        for t in range(2):
            window = early[:, t * T : (t + 1) * T]
            nc.scalar.activation(low[0][:, t, :], window.indirect(entries(0, HALF)), COPY)
            nc.vector.tensor_copy(low[1][:, t, :], window.indirect(entries(HALF, HALF)))
        for h in range(S // HALF):
            nc.scalar.activation(high[h][:, 0, :], early[:, 2 * T :].indirect(entries(h * HALF, HALF)), COPY)

        def quarter(tiles, i):
            h, c0 = divmod(i * QUARTER, HALF)
            return tiles[h][:, :, c0 : c0 + QUARTER]

        for i in reversed(quarters):
            weave(i, 0, quarter(low, i))
        for i in quarters[:-1]:
            nc.scalar.activation(quarter(high, i)[:, 1, :], last_plane[:].indirect(entries(i * QUARTER, QUARTER)), COPY)
        nc.vector.tensor_copy(quarter(high, 3)[:, 1, :], last_plane[:].indirect(entries(S - QUARTER, QUARTER)))
        order = (3, 0, 1, 2)
        for step, i in enumerate(order):
            weave(i, 1, quarter(high, i))
            if step > 0:
                quantize(order[step - 1])
        quantize(order[-1])

        products = []
        for i in quarters:
            y = psum.tile([N, QUARTER], F32, name=f"y{i}")
            nc.tensor.matmul_mx(out=y[:], lhsT=w_codes[:].bitcast(FP8X4), lhsT_scale=w_scales[:],
                                rhs=codes[:, i * QUARTER : (i + 1) * QUARTER].bitcast(FP8X4),
                                rhs_scale=scales[:, i * QUARTER : (i + 1) * QUARTER], start=True, stop=True)
            products.append(y)

        picked = held.tile([P, S], F32, name="picked")
        gates = held.tile([P, S], F32, name="gates")
        results = held.tile([P, S], F32, name="results")

        def cols(tile, first, count):
            return tile[:, first : first + count]

        def side_window(first, count):
            return side_rows[:].indirect(entries(first, count))

        nc.vector.tensor_tensor(cols(picked, 0, EIGHTH), side_window(0, EIGHTH), ones[:], MULT)
        for first, count in ((EIGHTH, EIGHTH), (QUARTER, QUARTER)):
            nc.scalar.activation(cols(picked, first, count), side_window(first, count), COPY)
        for i in quarters[2:]:
            nc.vector.tensor_copy(cols(picked, i * QUARTER, QUARTER), side_window(i * QUARTER, QUARTER))
        for i in quarters:
            nc.scalar.activation(cols(gates, i * QUARTER, QUARTER), cols(picked, i * QUARTER, QUARTER), SILU)
        for first, count in ((0, EIGHTH), (EIGHTH, EIGHTH)) + tuple((i * QUARTER, QUARTER) for i in quarters[1:]):
            i, c0 = divmod(first, QUARTER)
            nc.vector.tensor_tensor(cols(results, first, count), cols(products[i], c0, count),
                                    cols(gates, first, count), MULT)
            queue = nc.scalar if first == HALF else nc.sync
            queue.dma_start(out=cols(out, first, count), in_=cols(results, first, count))
